import numpy as np, ml_dtypes
CORES = [48,51,52,55]
N = 4
BF = ml_dtypes.bfloat16
def gentries(a):
    return np.ascontiguousarray(a.reshape(8, 16, -1).transpose(0, 2, 1)).reshape(8, -1)
def gtable(e):
    e = np.asarray(e); return np.ascontiguousarray(e.reshape(8, -1, 16).transpose(0, 2, 1)).reshape(128, -1).astype(np.int32)
S, K, W, C, RO = 256, 16, 4096, 16, 6
def H(e, v):
    return ((e * v >> 5) + e + 37 * v) & (W - 1)
def U(x, w):
    return np.add.reduce(x * w, axis=-1, dtype=np.int32) & (W - 1)
def applies(d, x, least):
    return np.add.reduce(d > x, axis=-1, dtype=np.int32) >= least
def parts(rng):
    lev = rng.choice(np.array([96, 160, 256]), (N, 8, 1, W))
    d = (rng.random((N, 8, 16, W)) * lev).astype(np.int64)
    return d, rng.integers(0, W, (N, 8, S, K)), rng.integers(0, 256, (N, 8, 16, S)), rng.integers(1, 256, (N, 8, 16))
def pack(d, e, z, w):
    return {"dv": d.reshape(N, 128, W).astype(np.float32).astype(BF), "ef": np.stack([gtable(a.reshape(8, -1)) for a in e]),
            "zv": z.reshape(N, 128, S).astype(np.float32).astype(BF), "wt": w.reshape(N, 128, 1).astype(np.int32)}
def stage(rng, d, w, r, g):
    o = rng.permutation(16); w[r, g] = 1; w[r, g, o[:8]] = 255
    m = np.zeros(16, np.int64); m[o[:4]] = 255; m[o[8:12]] = 255
    q = np.zeros(16, np.int64); q[rng.permutation(o[:15])[:9]] = 255
    row = int(o[15]); one = np.zeros(16, np.int64); one[row] = 255
    d[r, g, :, 0] = m; d[r, g, :, W - 1] = q; d[r, g, :, H(W - 1, 255 * 1024 & (W - 1))] = 255
    d[r, g, :, H(0, 255)] = m + one; d[r, g, :, H(W - 1, 255)] = q + one
    return row
def setup_inputs(rng):
    return pack(*parts(rng))
def setup_inputs_corners(rng):
    d, e, z, w = parts(rng); i = np.arange(S); kk = np.arange(K)
    for r in range(N):
        for g in range(8):
            if (r + g) % 2 == 1:
                stage(rng, d, w, r, g)
                few = np.argsort(np.argsort(rng.random((16, 64)), axis=0), axis=0) < np.where(np.arange(64) % 4 == 1, 0, 7)
                d[r, g, :, 16:80] = few * rng.integers(1, 256, (16, 64))
                goal = rng.choice(np.array([0, 1, 2, K - 2, K - 1]), S)[:, None]
                cold = rng.integers(16, 80, (S, K))
                v = np.where((kk < goal) | (goal == 0), cold, np.where(kk == goal, W - 1, e[r, g])); v[:, 0] = 0
                m = i % 4 != 3
                e[r, g] = np.where(m[:, None], v, e[r, g]); z[r, g] = np.where(m, 0, z[r, g])
            else:
                e[r, g, ::4] = e[r, g, ::4, :1]; e[r, g, 1::4] = (W - 1) * rng.integers(0, 2, e[r, g, 1::4].shape)
                z[r, g, :, 5::8] = 255; z[r, g, :, 6::8] = 0
    return pack(d, e, z, w)
def setup_inputs_ends(rng):
    p = rng.choice(np.array([0.0, 0.25, 0.5, 0.75, 0.9, 1.0]), (N, 8, 1, W)); d = 255 * (rng.random((N, 8, 16, W)) < p).astype(np.int64)
    d[..., 2::4] = rng.integers(0, 256, d[..., 2::4].shape)
    p = rng.choice(np.array([0.0, 0.1, 0.3, 0.5, 1.0]), (N, 8, 1, S)); z = 255 * (rng.random((N, 8, 16, S)) < p).astype(np.int64)
    z[..., 2::5] = rng.integers(0, 256, z[..., 2::5].shape)
    e = (W - 1) * rng.integers(0, 2, (N, 8, S, K)); w = np.where(rng.random((N, 8, 16)) < 0.5, 1, 255)
    for r in range(N):
        for g in range(8):
            if r < 2:
                row = stage(rng, d, w, r, g); z[r, g] = 0; z[r, g, row] = 255 * rng.integers(0, 2, S); z[r, g, row, 0] = 255; z[r, g, row, S - 1] = 0
                e[r, g, :, 0] = 0; e[r, g, :, 1:3] = 2 + 4 * rng.integers(0, W // 4, (S, 2)); e[r, g, :, K - 1] = W - 1
            elif (r == N - 1 and g == 7) or (r == N - 2 and g == 6):
                w[r, g] = 255; z[r, g, :, 1] = 255; z[r, g, :, S - 1] = 255; z[r, g, :, 3] = 0
            else:
                w[r, g, 13:15] = 1; w[r, g, 15] = 255
                for j in (1, S - 1):
                    z[r, g, :, j] = 0; z[r, g, 13:, j] = 255; e[r, g, j, 0] = W - 1; e[r, g, j, K - 1] = W - 1
    z[0, 7, :, S - 1] = 255
    return pack(d, e, z, w)
def setup_inputs_full(rng):
    d, e, z, w = parts(rng); i = np.arange(S); kk = np.arange(K); quiet = int(rng.integers(0, N)); turn = int(rng.integers(0, 8))
    for r in range(N):
        for g in range(8):
            kind = (5, 1, 5, 3)[g % 4] if r == quiet else (g + 3 * r + turn) % 8
            if kind == 1:
                o = np.argsort(np.argsort(rng.random((16, S)), axis=0), axis=0)
                z[r, g] = np.where(o < rng.integers(9, 17, S), 255, z[r, g])
            elif kind == 2:
                stage(rng, d, w, r, g)
                few = np.argsort(np.argsort(rng.random((16, 64)), axis=0), axis=0) < np.where(np.arange(64) % 4 == 1, 0, 7)
                d[r, g, :, 16:80] = few * rng.integers(1, 256, (16, 64))
                goal = rng.integers(4, K, S)[:, None]
                v = np.where(kk < goal, rng.integers(16, 80, (S, K)), np.where(kk == goal, W - 1, e[r, g])); v[:, 0] = 0
                m = i % 8 != 5
                e[r, g] = np.where(m[:, None], v, e[r, g]); z[r, g] = np.where(m, 0, z[r, g])
            elif kind == 3 or kind == 6:
                d[r, g] = rng.integers(160, 256, (16, W)); z[r, g] = rng.integers(100, 160, (16, S))
                if kind == 6: d[r, g] = np.where(rng.random(W) < 0.04, rng.integers(0, 100, (16, W)), d[r, g])
            elif kind == 4:
                w[r, g] = 255; half = (rng.permutation(16) < 8)[:, None]
                low = half ^ (rng.random(S) < 0.5)
                z[r, g] = np.where(low, rng.integers(0, 5, (16, S)), rng.integers(251, 256, (16, S)))
                t = rng.random(W); top = np.where(t < 0.3, half, np.where(t < 0.6, ~half, t < 0.85))
                v = np.where(top, rng.integers(251, 256, (16, W)), rng.integers(0, 5, (16, W)))
                d[r, g] = np.where((t >= 0.6) & (t < 0.85), 255, v)
            elif kind == 5:
                e[r, g] = e[r, g, :, :1]
            elif kind == 7:
                w[r, g] = 255; z[r, g] = rng.integers(244, 255, (16, S))
                o = np.argsort(np.argsort(rng.random((16, W)), axis=0), axis=0)
                d[r, g] = np.where((o < rng.integers(8, 17, W)) & (rng.random(W) < 0.6), 255, d[r, g])
    return pack(d, e, z, w)
def setup_inputs_spread(rng):
    d = (np.exp2(8 * rng.random((N, 8, 1, W))) * rng.random((N, 8, 16, W))).astype(np.int64)
    z = (np.exp2(8 * rng.random((N, 8, 1, S))) * rng.random((N, 8, 16, S))).astype(np.int64)
    e = np.minimum((np.exp2((W.bit_length() - 1) * rng.random((N, 8, S, K))) * rng.random((N, 8, S, K))).astype(np.int64), W - 1)
    e = np.where(rng.random((N, 8, S, 1)) < 0.5, W - 1 - e, e)
    w = np.minimum(1 + (np.exp2(8 * rng.random((N, 8, 16))) * rng.random((N, 8, 16))).astype(np.int64), 255)
    return pack(np.minimum(d, 255), e, np.minimum(z, 255), w)
def setup_inputs_ties(rng):
    d, e, z, w = parts(rng)
    d = rng.choice(np.array([0, 0, 100, 252]), (N, 8, 1, W)) + rng.integers(0, 4, d.shape)
    z = rng.choice(np.array([0, 100, 100, 252]), (N, 8, 1, S)) + rng.integers(0, 4, z.shape)
    e[:, :, ::4] = e[:, :, ::4, :1]; e[:, :, 1::4] = rng.choice(np.array([0, 1, W - 2, W - 1]), e[:, :, 1::4].shape)
    e[:, :, 2::4, K // 2:] = e[:, :, 2::4, :K // 2]
    return pack(d, e, z, w)
def check_inputs(d):
    bad = []
    for k, lo, hi in (("dv", 0, 255), ("ef", 0, W - 1), ("zv", 0, 255), ("wt", 1, 255)):
        x = np.asarray(d[k]).astype(np.float32)
        if not np.all((x >= lo) & (x <= hi) & (x == np.floor(x))): bad.append("range of " + k)
    return bad
def reference(dv, ef, zv, wt):
    g2 = np.arange(8)[:, None]; g3 = g2[:, :, None]; kk = np.arange(K - 1)
    D = [np.ascontiguousarray(a.astype(np.float32).astype(np.int32).reshape(8, 16, W).transpose(0, 2, 1)) for a in dv]
    E = [gentries(a).astype(np.int32).reshape(8, S, K) for a in ef]
    z = [np.ascontiguousarray(a.astype(np.float32).astype(np.int32).reshape(8, 16, S).transpose(0, 2, 1)) for a in zv]
    w = wt.astype(np.int32).reshape(N, 8, 1, 1, 16)
    A = [0] * N
    for t in range(RO):
        name = []
        for r in range(N):
            least = 8 + (A[r] & 1); e = E[r]; x = z[r][:, :, None, :]
            n = H(e, U(x, w[r]))
            d = D[r][g3, n]
            a = applies(d, x, least)
            zk = np.where(a[..., None], np.abs(x - d), x); z0 = zk[:, :, :1]
            b = applies(D[r][g3, H(e[:, :, :1], U(zk, w[r]))], zk, least)
            c = applies(D[r][g3, H(e, U(z0, w[r]))], z0, least)
            ok = (b != a[:, :, :1]) & (c == a); ok[:, :, 0] = False
            s = np.argmax(ok, axis=2)
            name.append(np.take_along_axis(n, s[:, :, None], 2)[:, :, 0])
            z[r] = np.take_along_axis(zk, s[:, :, None, None], 2)[:, :, 0]
            E[r] = np.concatenate([np.take_along_axis(e, kk + (kk >= s[:, :, None]), 2), np.zeros((8, S, 1), np.int32)], axis=2)
            A[r] = int(np.count_nonzero(s))
        for r in range(N):
            q = (r - 1 - t % (N - 1)) % N
            E[r][:, :, K - 1] = name[q]
            col = C * np.arange(S) + (name[q] & (C - 1))
            D[r][g2, col] = (D[r][g2, col] + z[q]) >> 1
    return {"yd": np.stack([a.transpose(0, 2, 1).reshape(128, W) for a in D]).astype(np.float32).astype(BF),
            "ye": np.stack([gtable(a.reshape(8, -1)) for a in E]).astype(np.float32),
            "yz": np.stack([a.transpose(0, 2, 1).reshape(128, S) for a in z]).astype(np.float32).astype(BF)}

import numpy as np
from concourse.mybir import dt, AluOpType, AxisListType, ActivationFunctionType

RO = 6
BIG = 2.0 ** 18
A_S = ((12, 14), (14, 16))
A_V = ((0, 1), (1, 3), (3, 5), (5, 7), (7, 9), (9, 11), (11, 12))
M_S = ()
A_C = ((1, 9, 0), (9, 16, 0))
C_C = ((1, 9, 1), (9, 16, 1))
C_H = ((1, 5), (5, 16))
B_H = ((1, 9), (9, 16))
B_C = ((1, 9, 0), (9, 16, 0))

SCRATCH = {
    "XI": ("sbuf", [128, 8, 32], "int32"), "XJ": ("sbuf", [128, 8, 32], "int32"),
    "YI": ("sbuf", [128, 8, 32], "float32"), "YJ": ("sbuf", [128, 8, 32], "float32"),
    "XF": ("sbuf", [128, 256], "float32"), "RT": ("sbuf", [128, 256], "float32"),
    "wti": ("sbuf", [128, 1], "int32"), "wtf": ("sbuf", [128, 1], "float32"),
    "DD": ("sbuf", [128, 4096], "bfloat16"),
    "AB0": ("sbuf", [128, 5120], "bfloat16"), "AB1": ("sbuf", [128, 5120], "bfloat16"),
    "df0": ("sbuf", [128, 4096], "bfloat16"), "df1": ("sbuf", [128, 4096], "bfloat16"),
    "ma": ("sbuf", [128, 4096], "bfloat16"), "mb": ("sbuf", [128, 4096], "bfloat16"), "mc": ("sbuf", [128, 4096], "bfloat16"),
    "dg": ("sbuf", [128, 4096], "bfloat16"), "dc": ("sbuf", [128, 4096], "bfloat16"),
    "db": ("sbuf", [128, 4096], "bfloat16"),
    "OV": ("sbuf", [128, 2048], "bfloat16"), "OS": ("sbuf", [128, 2048], "bfloat16"), "WW": ("sbuf", [128, 2048], "bfloat16"),
    "on8": ("sbuf", [128, 8], "float32"), "b8a": ("sbuf", [128, 8], "float32"), "b8": ("sbuf", [128, 8], "float32"),
    "wb8": ("sbuf", [128, 8], "float32"), "on16": ("sbuf", [128, 16], "float32"),
    "one": ("sbuf", [128, 256], "bfloat16"), "ID": ("sbuf", [128, 128], "bfloat16"), "nID": ("sbuf", [128, 128], "bfloat16"),
    "I22": ("sbuf", [128, 128], "bfloat16"), "IP": ("sbuf", [128, 128], "bfloat16"), "IN": ("sbuf", [128, 128], "bfloat16"),
    "NBV": ("sbuf", [128, 128], "bfloat16"), "NBS": ("sbuf", [128, 128], "bfloat16"),
    "KC": ("sbuf", [128, 256], "bfloat16"), "KI": ("sbuf", [128, 256], "float32"),
    "sl": ("sbuf", [128, 16], "int32"), "sl16": ("sbuf", [128, 16], "int32"), "it0": ("sbuf", [128, 16], "int32"),
    "it1": ("sbuf", [128, 16], "int32"), "it2": ("sbuf", [128, 16], "int32"),
    "EB0": ("sbuf", [128, 272], "float32"), "EB1": ("sbuf", [128, 272], "float32"),
    "y1": ("sbuf", [128, 256], "float32"),
    "ui": ("sbuf", [128, 64], "int32"), "va": ("sbuf", [128, 64], "int32"), "vx": ("sbuf", [128, 64], "float32"),
    "x1": ("sbuf", [128, 256], "float32"), "x2": ("sbuf", [128, 256], "int32"), "nn": ("sbuf", [128, 256], "int32"),
    "nu": ("sbuf", [128, 256], "uint16"),
    "uic": ("sbuf", [128, 16], "int32"), "vac": ("sbuf", [128, 16], "int32"), "vxc": ("sbuf", [128, 64], "float32"),
    "x1c": ("sbuf", [128, 256], "float32"), "x2c": ("sbuf", [128, 256], "int32"), "nc": ("sbuf", [128, 256], "int32"),
    "ncu": ("sbuf", [128, 256], "uint16"),
    "uib": ("sbuf", [128, 256], "int32"), "vab": ("sbuf", [128, 256], "int32"), "vxb": ("sbuf", [128, 256], "float32"),
    "x1b": ("sbuf", [128, 256], "float32"), "x2b": ("sbuf", [128, 256], "int32"), "nb": ("sbuf", [128, 256], "int32"),
    "nbu": ("sbuf", [128, 256], "uint16"),
    "na0": ("sbuf", [128, 16], "bfloat16"), "nax": ("sbuf", [128, 256], "bfloat16"), "s0": ("sbuf", [128, 256], "bfloat16"),
    "q0": ("sbuf", [128, 256], "float32"), "q1": ("sbuf", [128, 256], "float32"), "q2": ("sbuf", [128, 256], "float32"),
    "c0": ("sbuf", [128, 16], "float32"), "c1": ("sbuf", [128, 16], "float32"),
    "cd": ("sbuf", [128, 256], "float32"), "tr": ("sbuf", [128, 128], "float32"),
    "t64": ("sbuf", [128, 64], "float32"), "t32": ("sbuf", [128, 32], "float32"), "ci": ("sbuf", [128, 16], "int32"),
    "m1": ("sbuf", [128, 16], "int32"), "m2": ("sbuf", [128, 16], "int32"), "mu": ("sbuf", [128, 16], "uint16"),
    "g0": ("sbuf", [128, 16], "bfloat16"), "gj": ("sbuf", [128, 16], "float32"), "ac": ("sbuf", [128, 1], "float32"),
    "ai": ("sbuf", [128, 1], "int32"), "ap1": ("sbuf", [128, 1], "int32"), "tb": ("sbuf", [128, 1], "float32"),
    "tb2": ("sbuf", [128, 1], "float32"),
    "kp": ("sbuf", [128, 16], "int32"), "lt": ("sbuf", [128, 16], "float32"), "th": ("sbuf", [128, 64], "bfloat16"),
    "k1": ("sbuf", [128, 16], "int32"), "k2": ("sbuf", [128, 16], "int32"), "cu": ("sbuf", [128, 16], "uint16"),
    "ds": ("sbuf", [128, 256], "int32"), "dh": ("sbuf", [128, 256], "int32"),
    "pE": ("psum", [128, 512], "float32"), "pF": ("psum", [128, 512], "float32"), "pA": ("psum", [128, 512], "float32"),
    "pU": ("psum", [128, 512], "float32"), "pB": ("psum", [128, 512], "float32"), "pC": ("psum", [128, 512], "float32"),
    "pG": ("psum", [128, 512], "float32"), "pH": ("psum", [128, 512], "float32"),
}
for _t in range(RO):
    SCRATCH["zl%d" % _t] = ("sbuf", [128, 256], "bfloat16")
    SCRATCH["nl%d" % _t] = ("sbuf", [128, 16], "int32")
    SCRATCH["ns%d" % _t] = ("sbuf", [128, 16], "int32")
PSUM = ("pE", "pF", "pA", "pU", "pB", "pC", "pG", "pH")
SEMAPHORES = ["qv", "qs", "qt", "qg"]
for _t in range(RO):
    SEMAPHORES += ["an%d" % _t, "az%d" % _t, "ln%d" % _t, "lz%d" % _t]
SEMAPHORES += ["dm%d" % _i for _i in range(40)]

BONUS = {"ca": -8000, "m0": 12000, "de": -8000, "b": -8000, "hc": 12000, "am": 2000, "hs": 2000, "a0": 8000, "hb": 0, "qu": 16000,
         "nm": 8000, "up": 4000, "q0": 12000, "as": 2000, "tl": -2000, "h2": 2000}
CY = 0.83 * 1.25
GA = 1.56
CT = 0.42 * 1.2
WAKE = 60.0
NET_N, NET_Z = 2200.0, 2600.0


def build(T, core, topo):
    A = AluOpType
    F = ActivationFunctionType
    rank = T.rank_of(core)
    ops = []
    ndma = [0]
    cls = ["-"]

    def ap(r):
        if len(r) == 4:
            return T[r[0]][:, r[1]:r[2]:r[3]]
        return T[r[0]][:, r[1]:r[2]]

    def add(q, fn, rd, wr, cost, kind="c", lat=0.0, sem=None, after=None):
        ops.append({"q": q, "fn": fn, "rd": [r[:3] for r in rd], "wr": [r[:3] for r in wr], "cost": cost, "kind": kind,
                    "lat": lat, "sem": sem, "after": after, "cls": cls[0]})
        return len(ops) - 1

    def width(r):
        return len(range(*r[1:])) if len(r) == 4 else r[2] - r[1]

    def two(*rs):
        return all(r[0] not in PSUM and SCRATCH[r[0]][2] in ("bfloat16", "uint16") for r in rs)

    def cost1(n, fast):
        return 55 + CY * max(64, n * (0.5 if fast else 1.0))

    def tt(o, a, b, op):
        f = 1 if (a[0] in PSUM or b[0] in PSUM) else 2
        add("v", lambda e: e.tensor_tensor(ap(o), ap(a), ap(b), op), [a, b], [o], 55 + CY * max(64, f * width(o)))

    def ts(o, a, s1, op0, s2=None, op1=None):
        rd = [a]
        v1 = s1
        if isinstance(s1, tuple):
            rd.append(s1)
        if op1 is None:
            add("v", lambda e: e.tensor_scalar(ap(o), ap(a), ap(s1) if isinstance(s1, tuple) else s1, None, op0), rd, [o],
                cost1(width(o), two(o, a)))
        else:
            add("v", lambda e: e.tensor_scalar(ap(o), ap(a), ap(s1) if isinstance(s1, tuple) else s1, s2, op0, op1), rd, [o],
                cost1(width(o), two(o, a)))

    def cp(o, a):
        add("v", lambda e: e.tensor_copy(ap(o), ap(a)), [a], [o], cost1(width(o), two(o, a)))

    def fill(o, c):
        add("v", lambda e: e.memset(ap(o), c), [], [o], cost1(width(o), two(o)))

    def gtt(o, win, off, b, op):
        add("v", lambda e: e.tensor_tensor(ap(o), ap(win).indirect(ap(off)), ap(b), op), [win, off, b], [o],
            50 + CY * GA * width(o))

    def gcp(o, win, off):
        add("v", lambda e: e.tensor_copy(ap(o), ap(win).indirect(ap(off))), [win, off], [o], 50 + CY * GA * width(o))

    def scat(win, off, a):
        add("v", lambda e: e.tensor_copy(ap(win).indirect(ap(off)), ap(a)), [off, a], [win], 50 + CY * 3.5 * width(a))

    def act(o, a, func, bias=None, scale=None, acc=None):
        kw = {}
        rd = [a]
        if bias is not None:
            kw["bias"] = bias
        sc = isinstance(scale, tuple)
        if sc:
            rd.append(scale)

        def fn(e):
            k = dict(kw)
            if scale is not None:
                k["scale"] = ap(scale) if sc else scale
            if acc is not None:
                k["accum_out"] = ap(acc)
            return e.activation(ap(o), ap(a), func, **k)
        add("s", fn, rd, [o] + ([acc] if acc is not None else []), 80 + CY * max(64, width(o)))

    def gact(o, win, off):
        add("s", lambda e: e.activation(ap(o), ap(win).indirect(ap(off)), F.Copy), [win, off], [o], 65 + CY * GA * width(o))

    def mms(lst):
        def fn(e):
            r = None
            for o, l, x, st, sp in lst:
                r = e.matmul(ap(o), ap(l), ap(x), st, sp)
            return r
        wr = {}
        for o, l, x, st, sp in lst:
            lo, hi = wr.get(o[0], (o[1], o[2]))
            wr[o[0]] = (min(lo, o[1]), max(hi, o[2]))
        rd = {}
        for o, l, x, st, sp in lst:
            for y in (l, x):
                lo, hi = rd.get(y[0], (y[1], y[2]))
                rd[y[0]] = (min(lo, y[1]), max(hi, y[2]))
        add("t", fn, [(k, v[0], v[1]) for k, v in rd.items()], [(k, v[0], v[1]) for k, v in wr.items()],
            60 + CT * sum(max(64, width(x)) for o, l, x, st, sp in lst))

    def sums(o, mat, buf, lo, hi, extra=()):
        lst = [(o, (mat, 128 * p, 128 * p + 128), (buf, lo + p, hi, 16)) for p in range(16)] + [(o, l, x) for l, x in extra]
        mms([(a, b, c, i == 0, i == len(lst) - 1) for i, (a, b, c) in enumerate(lst)])

    def gop(fn, rd, wr, cost):
        add("g", fn, rd, wr, cost)

    def dma(q, out_fn, in_fn, rd, wr, lat):
        s = "dm%d" % ndma[0]
        ndma[0] += 1
        return add(q, lambda e: e.dma_start(out_fn(), in_fn()), rd, wr, 70.0, kind="dma", lat=lat, sem=s)

    def send(t, what, src, dstname, dst, cost, lat):
        rid, pid, _e = topo.addr(dst)
        m = topo.mask(core, dst)
        i = add("g", lambda e: e.remote_dma(T[dstname][:, 0:SCRATCH[dstname][1][1]], ap(src), T.sem["a%s%d" % (what, t)],
                                            T.sem["l%s%d" % (what, t)], pid, rid, m), [src], [], cost, kind="send", lat=lat,
                sem="l%s%d" % (what, t))
        return i

    def arrive(t, what, dstname, after, lat):
        add("n%d%s" % (t, what), None, [], [(dstname, 0, SCRATCH[dstname][1][1])], lat, kind="arr", sem="a%s%d" % (what, t),
            after=after)

    IDr = ("ID", 0, 128)

    dma("y", lambda: T.wti[:, 0:1], lambda: T.wt[:, 0:1], [], [("wti", 0, 1)], 1900)
    dma("y", lambda: T.XI[:], lambda: T.ef[:], [], [("XI", 0, 256)], 2000)
    dma("y", lambda: T.AB0[:, 768:1024], lambda: T.zv[:], [], [("AB0", 768, 1024)], 2000)
    dma("s", lambda: T.XJ[:], lambda: T.ef[:], [], [("XJ", 0, 256)], 2000)
    dma("s", lambda: T.DD[:], lambda: T.dv[:], [], [("DD", 0, 4096)], 5000)

    def swap(q, dst, src, gi, h, dd):
        o = gi ^ 1
        dma(q, lambda: T[dst][16 * gi:16 * gi + 16, :, 16 * (1 - h):16 * (1 - h) + 16],
            lambda: T[src][16 * o:16 * o + 16, :, 16 * h:16 * h + 16], [(src, 0, 256)], [(dst, 32 * gi + 1000, 32 * gi + 1032)], 1900)
    ops[3]["wr"].append(("XJ", 1000, 1256))
    for gi in range(8):
        swap("y" if gi % 2 else "s", "XJ", "XI", gi, gi % 2, None)

    fill(("on8", 0, 8), 1.0)
    fill(("one", 0, 256), 1.0)
    gop(lambda e: e.affine_select(T.b8a[:, 0:8], T.on8[:, 0:8], [[-16, 8]], A.is_ge, 0.0, 0, 1), [("on8", 0, 8)], [("b8a", 0, 8)], 190)
    gop(lambda e: e.affine_select(T.b8[:, 0:8], T.b8a[:, 0:8], [[16, 8]], A.is_ge, 0.0, 15, -1), [("b8a", 0, 8)], [("b8", 0, 8)], 190)
    gop(lambda e: e.affine_select(T.ID[:, 0:128], T.one[:, 0:128], [[-1, 128]], A.is_equal, 0.0, 0, 1), [("one", 0, 128)], [IDr], 400)
    gop(lambda e: e.iota(T.KI[:, 0:256], [[1, 16], [0, 16]], 4, 0, allow_small_or_imprecise_dtypes=True), [], [("KI", 0, 256)], 600)
    gop(lambda e: e.iota(T.it0[:, 0:16], [[0, 16]], 0, 1), [], [("it0", 0, 16)], 180)
    gop(lambda e: e.iota(T.it1[:, 0:16], [[16, 16]], 0, 0), [], [("it1", 0, 16)], 180)
    fill(("WW", 0, 2048), 0.0)
    fill(("OV", 0, 2048), 0.0)
    fill(("on16", 0, 16), 1.0)
    cp(("wtf", 0, 1), ("wti", 0, 1))
    ts(("wb8", 0, 8), ("b8", 0, 8), ("wtf", 0, 1), A.mult)
    for j in range(8):
        act(("WW", 16 * j, 16 * j + 1936, 129), ("on16", 0, 16), F.Copy, scale=("wb8", j, j + 1))
        ops[-1]["wr"] = [("WW", 3000 + j, 3001 + j)]
        ops[-1]["rd"] += [("WW", 0, 2048)]
        ts(("OV", 16 * j, 16 * j + 1936, 129), ("on16", 0, 16), ("b8", j, j + 1), A.mult, BIG, A.mult)
        ops[-1]["wr"] = [("OV", 3000 + j, 3001 + j)]
        ops[-1]["rd"] += [("OV", 0, 2048)]
    act(("OS", 0, 2048), ("OV", 0, 2048), F.Copy, scale=0.5)
    ops[-1]["rd"] += [("OV", 3000, 3008)]
    ts(("nID", 0, 128), IDr, -1.0, A.mult)
    ts(("I22", 0, 128), IDr, 2.0 ** 22, A.mult)
    ts(("IP", 0, 128), IDr, 2.0 ** 14, A.mult)
    ts(("IN", 0, 128), IDr, -2.0 ** 14, A.mult)
    ts(("pC", 256, 512), ("KI", 0, 256), 4096.0, A.mult)
    fill(("pC", 256, 272), 3 * 4096.0)
    ts(("KC", 0, 256), ("KI", 0, 256), -0.5, A.add)
    fill(("KC", 0, 16), 23.5)
    ts(("it2", 0, 16), ("it0", 0, 16), 15, A.bitwise_and)
    tt(("sl", 0, 16), ("it2", 0, 16), ("it1", 0, 16), A.add)
    ts(("sl16", 0, 16), ("sl", 0, 16), 16, A.mult)
    fill(("tb", 0, 1), -7.5 * BIG)

    def bias_mats():
        act(("tb2", 0, 1), ("tb", 0, 1), F.Identity, bias=8.0 * BIG)
        act(("NBV", 0, 128), IDr, F.Copy, scale=("tb", 0, 1))
        act(("NBS", 0, 128), IDr, F.Copy, scale=("tb2", 0, 1))
    bias_mats()
    for b in range(8):
        add("v", (lambda b: lambda e: e.tensor_scalar(T.XF[:, 32 * b:32 * b + 32], T.XJ[:, b], 1184.0, None, A.add))(b),
            [("XJ", 0, 256), ("XJ", 1000, 1256)], [("XF", 32 * b, 32 * b + 32)], cost1(32, False))
    add("v", lambda e: e.transpose(T.RT[:, 0:256], T.XF[:, 0:256]), [("XF", 0, 256)], [("RT", 0, 256)], cost1(256, False))

    def blk(k):
        return 0 if k == 0 else 16 - k
    for k in range(16):
        b = blk(k)
        o, a = ("EB0", 16 + 16 * b, 32 + 16 * b), ("RT", k, 256, 16)
        if k % 2:
            act(o, a, F.Copy)
        else:
            cp(o, a)
    act(("EB0", 0, 16), ("RT", 1, 256, 16), F.Copy)

    def wrefs(mat):
        ops[-1]["rd"].append((mat, 3000, 3008))
    C2 = -6722560.0

    def effects(eb):
        act(("pE", 0, 256), (eb, 16, 272), F.Copy)
        act(("pF", 0, 256), (eb, 16, 272), F.Identity, bias=C2, scale=2080.0)

    def first_effect(eb):
        act(("pE", 272, 288), (eb, 16, 32), F.Copy)
        act(("pE", 288, 304), (eb, 16, 32), F.Copy)
        act(("pE", 304, 336), ("pE", 272, 304), F.Copy)
        act(("pE", 336, 400), ("pE", 272, 336), F.Copy)
        act(("pE", 400, 512), ("pE", 272, 384), F.Copy)
        act(("pF", 272, 512), ("pE", 272, 512), F.Identity, bias=C2, scale=2080.0)

    for t in range(RO):
        AB, AN = "AB%d" % (t % 2), "AB%d" % ((t + 1) % 2)
        EB, EN = "EB%d" % (t % 2), "EB%d" % ((t + 1) % 2)
        DF = "df%d" % (t % 2)
        D = ("DD", 0, 4096)
        cls[0] = "hs"
        act((AB, 512, 768), (AB, 768, 1024), F.Copy)
        act((AB, 0, 512), (AB, 512, 1024), F.Copy)
        sums(("pU", 256, 320), "WW", AB, 0, 1024)
        wrefs("WW")
        cp(("ui", 0, 64), ("pU", 256, 320))
        ts(("va", 0, 64), ("ui", 0, 64), 4095, A.bitwise_and)
        ts(("vx", 0, 64), ("va", 0, 64), -2048.0, A.add)
        if t > 0:
            nl = ("nl%d" % (t - 1), 0, 16)
            ts((EB, 32, 48), nl, 1184.0, A.add)
            ts(("k1", 0, 16), nl, 15, A.bitwise_and)
            tt(("k2", 0, 16), ("k1", 0, 16), ("sl16", 0, 16), A.add)
            cp(("cu", 0, 16), ("k2", 0, 16))
        cls[0] = "ef"
        effects(EB)
        first_effect(EB)
        cls[0] = "hs"
        for j in range(4):
            tt(("x1", 64 * j, 64 * j + 64), ("pE", 64 * j, 64 * j + 64), ("vx", 0, 64), A.mult)
        tt(("x2", 0, 256), ("pF", 0, 256), ("x1", 0, 256), A.add)
        ts(("nn", 0, 256), ("x2", 0, 256), 5, A.arith_shift_right, 4095, A.bitwise_and)
        cp(("nu", 0, 256), ("nn", 0, 256))
        cls[0] = "q0"
        tt(("q0", 0, 256), ("pC", 256, 512), ("nn", 0, 256), A.add)
        cls[0] = "up"
        if t > 0:
            gtt(("ds", 0, 256), D, ("cu", 0, 16), ("zl%d" % (t - 1), 0, 256), A.add)
            ts(("dh", 0, 256), ("ds", 0, 256), 1, A.arith_shift_right)
            scat(D, ("cu", 0, 16), ("dh", 0, 256))

        def gather_a(lo, hi):
            gtt((DF, 256 * lo, 256 * hi), D, ("nu", 16 * lo, 16 * hi), (AB, 1024 - 256 * (hi - lo), 1024), A.subtract)

        def absd(lo, hi):
            act((AB, 1024 + 256 * lo, 1024 + 256 * hi), (DF, 256 * lo, 256 * hi), F.Abs)

        def mask_a(lo, hi):
            if lo in M_S:
                act(("ma", 256 * lo, 256 * hi), (DF, 256 * lo, 256 * hi), F.Sign, bias=-0.5)
            else:
                ts(("ma", 256 * lo, 256 * hi), (DF, 256 * lo, 256 * hi), 0.0, A.is_gt)

        def count(bank, buf, lo, hi, sgn, extra=()):
            if sgn:
                sums((bank, 16 * lo, 16 * hi), "OS", buf, 256 * lo, 256 * hi, [(("NBS", 0, 128), ("one", 0, 16 * (hi - lo)))] + list(extra))
            else:
                sums((bank, 16 * lo, 16 * hi), "OV", buf, 256 * lo, 256 * hi, [(("NBV", 0, 128), ("one", 0, 16 * (hi - lo)))] + list(extra))
                wrefs("OV")

        def sums_u(lo, hi):
            sums(("pU", 16 * lo, 16 * hi), "WW", AB, 1024 + 256 * lo, 1024 + 256 * hi)
            wrefs("WW")
        cls[0] = "a0"
        gather_a(0, 1)
        absd(0, 1)
        sums_u(0, 1)
        cls[0] = "m0"
        mask_a(0, 1)
        count("pA", "ma", 0, 1, 0 in M_S)
        cls[0] = "hc"
        cp(("uic", 0, 16), ("pU", 0, 16))
        ts(("vac", 0, 16), ("uic", 0, 16), 4095, A.bitwise_and)
        ts(("vxc", 0, 16), ("vac", 0, 16), -2048.0, A.add)
        cp(("vxc", 16, 32), ("vxc", 0, 16))
        cp(("vxc", 32, 64), ("vxc", 0, 32))
        for c, d in C_H:
            for lo in range(c, d, 4):
                hi = min(lo + 4, d)
                tt(("x1c", 16 * lo, 16 * hi), ("pE", 16 * lo, 16 * hi), ("vxc", 0, 16 * (hi - lo)), A.mult)
            c, d = 16 * c, 16 * d
            tt(("x2c", c, d), ("pF", c, d), ("x1c", c, d), A.add)
            ts(("nc", c, d), ("x2c", c, d), 5, A.arith_shift_right, 4095, A.bitwise_and)
            cp(("ncu", c, d), ("nc", c, d))
            cls[0] = "h2"
        cls[0] = "m0"
        ts(("na0", 0, 16), ("pA", 0, 16), 0.0, A.is_lt)
        mms([(("pA", 256 + 16 * b, 272 + 16 * b), IDr, ("na0", 0, 16), True, True) for b in range(1, 16)])
        act(("nax", 16, 256), ("pA", 272, 512), F.Copy)
        act(("s0", 16, 256), ("nax", 16, 256), F.Identity, bias=-1.0, scale=2.0)
        ts(("c0", 0, 16), ("na0", 0, 16), -4096.0, A.mult, 4096.0, A.add)
        tt(("c1", 0, 16), ("c0", 0, 16), ("q0", 0, 16), A.add)
        nslot = [0]

        def apart(buf, off, lo, hi, other):
            bank = ("pG", "pH")[nslot[0] % 2]
            nslot[0] += 1
            gact((buf, 256 * lo, 256 * hi), D, (off, 16 * lo, 16 * hi))
            for i, b in enumerate(range(lo, hi)):
                mms([((bank, 256 * i, 256 * i + 256), IDr, (buf, 256 * b, 256 * b + 256), True, False),
                     ((bank, 256 * i, 256 * i + 256), ("nID", 0, 128), other(b), False, True)])
            return (bank, 0, 256 * (hi - lo))
        for lo, hi in A_S:
            cls[0] = "as"
            p = apart("dg", "nu", lo, hi, lambda b: (AB, 768, 1024))
            act((AB, 1024 + 256 * lo, 1024 + 256 * hi), p, F.Abs)
            if lo in M_S:
                act(("ma", 256 * lo, 256 * hi), p, F.Sign, bias=-0.5)
            else:
                ts(("ma", 256 * lo, 256 * hi), p, 0.0, A.is_gt)
        for lo, hi in A_V[1:]:
            cls[0] = "av"
            gather_a(lo, hi)
            absd(lo, hi)
            cls[0] = "am"
            mask_a(lo, hi)

        def hash_b(lo, hi):
            c = 16 * lo
            d = 16 * hi
            sums_u(lo, hi)
            cp(("uib", c, d), ("pU", c, d))
            ts(("vab", c, d), ("uib", c, d), 4095, A.bitwise_and)
            ts(("vxb", c, d), ("vab", c, d), -2048.0, A.add)
            tt(("x1b", c, d), ("pE", 256 + c, 256 + d), ("vxb", c, d), A.mult)
            tt(("x2b", c, d), ("pF", 256 + c, 256 + d), ("x1b", c, d), A.add)
            ts(("nb", c, d), ("x2b", c, d), 5, A.arith_shift_right, 4095, A.bitwise_and)
            cp(("nbu", c, d), ("nb", c, d))
        cls[0] = "cs"
        for lo, hi, sgn in C_C:
            if sgn:
                for b in range(lo, hi, 2):
                    p = apart("dc", "ncu", b, min(b + 2, hi), lambda b: (AB, 1024, 1280))
                    act(("mc", 256 * b, 256 * min(b + 2, hi)), p, F.Sign, bias=-0.5)
            else:
                for b in range(lo, hi):
                    gtt(("mc", 256 * b, 256 * b + 256), D, ("ncu", 16 * b, 16 * b + 16), (AB, 1024, 1280), A.is_gt)
            count("pC", "mc", lo, hi, sgn, [(("I22", 0, 128), ("nax", 16 * lo, 16 * hi))])
        for lo, hi in B_H:
            cls[0] = "hb"
            hash_b(lo, hi)
            cls[0] = "b"
            for c, d, sgn in B_C:
                if c < lo or c >= hi:
                    continue
                st = 2 if sgn else 4
                for q in range(c, d, st):
                    r = min(q + st, d)
                    if sgn:
                        p = apart("db", "nbu", q, r, lambda b: (AB, 1024 + 256 * b, 1280 + 256 * b))
                        act(("mb", 256 * q, 256 * r), p, F.Sign, bias=-0.5)
                    else:
                        gtt(("mb", 256 * q, 256 * r), D, ("nbu", 16 * q, 16 * r), (AB, 1024 + 256 * q, 1024 + 256 * r), A.is_gt)
        cls[0] = "ca"
        for lo, hi, sgn in A_C:
            count("pA", "ma", lo, hi, sgn)
        for lo, hi in B_H:
            tt(("q1", 16 * lo, 16 * hi), ("pA", 16 * lo, 16 * hi), ("q0", 16 * lo, 16 * hi), A.min)
        cls[0] = "de"
        for lo, hi in B_H:
            c = 16 * lo
            d = 16 * hi
            tt(("q2", c, d), ("pC", c, d), ("q1", c, d), A.min)
        for lo, hi, sgn in B_C:
            c = 16 * lo
            d = 16 * hi
            count("pB", "mb", lo, hi, sgn)
            z = ("pU", 256 + c, 256 + d)
            tt(z, ("pB", c, d), ("s0", c, d), A.mult)
            tt(("cd", c, d) if lo < 9 else z, z, ("q2", c, d), A.min)
        cls[0] = "tl"
        tt(("tr", 112, 128), ("c1", 0, 16), ("cd", 128, 144), A.max)
        tt(("tr", 0, 112), ("pU", 400, 512), ("cd", 16, 128), A.max)
        tt(("t64", 0, 64), ("tr", 0, 64), ("tr", 64, 128), A.max)
        tt(("t32", 0, 32), ("t64", 0, 32), ("t64", 32, 64), A.max)
        tt(("ci", 0, 16), ("t32", 0, 16), ("t32", 16, 32), A.max)
        ns = "ns%d" % t
        dst = T.cores[(rank + 1 + t % 3) % len(T.cores)]
        ts((ns, 0, 16), ("ci", 0, 16), 4095, A.bitwise_and)
        i = send(t, "n", (ns, 0, 16), "nl%d" % t, dst, 900.0, 1500.0)
        arrive(t, "n", "nl%d" % t, i, NET_N)
        ts(("m1", 0, 16), ("ci", 0, 16), 4, A.arith_shift_right, 0x1F00, A.bitwise_and)
        tt(("m2", 0, 16), ("m1", 0, 16), ("sl", 0, 16), A.add)
        cp(("mu", 0, 16), ("m2", 0, 16))
        gcp((AN, 768, 1024), (AB, 0, 5120), ("mu", 0, 16))
        i = send(t, "z", (AN, 768, 1024), "zl%d" % t, dst, 900.0, 1700.0)
        arrive(t, "z", "zl%d" % t, i, NET_Z)
        if t == RO - 1:
            dma("y", lambda: T.yz[:], lambda: T[AN][:, 768:1024], [(AN, 768, 1024)], [], 2000)
        cls[0] = "nt"
        if t < RO - 1:
            ts(("g0", 0, 16), ("ci", 0, 16), 20480.0, A.is_ge)
            mms([(("pU", 384, 400), ("one", 0, 128), ("g0", 0, 16), True, True)])
            act(("gj", 0, 16), ("pU", 384, 400), F.Copy, acc=("ac", 0, 1))
            cp(("ai", 0, 1), ("ac", 0, 1))
            ts(("ap1", 0, 1), ("ai", 0, 1), 1, A.bitwise_and)
            ts(("tb", 0, 1), ("ap1", 0, 1), -BIG, A.mult, -7.5 * BIG, A.add)
            bias_mats()
        cls[0] = "qu"
        ts(("kp", 0, 16), ("ci", 0, 16), 12, A.arith_shift_right)
        ts(("lt", 0, 16), ("ci", 0, 16), 20480.0, A.is_lt, 32.0, A.mult)
        tt(("th", 0, 16), ("kp", 0, 16), ("lt", 0, 16), A.max)
        act(("th", 16, 32), ("th", 0, 16), F.Copy)
        act(("th", 32, 64), ("th", 0, 32), F.Copy)
        for off, m, n in ((0, "IP", "IN"), (256, "IN", "IP")):
            lst = []
            for b in range(0, 256, 64):
                o = ("pB", off + b, off + b + 64)
                lst.append((o, (m, 0, 128), ("KC", b, b + 64), True, False))
                lst.append((o, (n, 0, 128), ("th", 0, 64), False, True))
            mms(lst)
        tt(("y1", 0, 256), ("pB", 0, 256), (EB, 16, 272), A.min)
        tt(("pB", 256, 512), ("pB", 256, 512), (EB, 0, 256), A.min)
        tt((EN, 16, 32), ("pB", 256, 272), ("y1", 0, 16), A.max)
        tt((EN, 48, 272), ("pB", 288, 512), ("y1", 32, 256), A.max)
        act((EN, 0, 16), (EN, 256, 272), F.Copy)

    cls[0] = "up"
    nl = ("nl%d" % (RO - 1), 0, 16)
    EB = "EB%d" % (RO % 2)
    D = ("DD", 0, 4096)
    ts(("k1", 0, 16), nl, 15, A.bitwise_and)
    tt(("k2", 0, 16), ("k1", 0, 16), ("sl16", 0, 16), A.add)
    cp(("cu", 0, 16), ("k2", 0, 16))
    ts((EB, 32, 48), nl, 1184.0, A.add)
    gtt(("ds", 0, 256), D, ("cu", 0, 16), ("zl%d" % (RO - 1), 0, 256), A.add)
    ts(("dh", 0, 256), ("ds", 0, 256), 1, A.arith_shift_right)
    scat(D, ("cu", 0, 16), ("dh", 0, 256))
    dma("s", lambda: T.yd[:], lambda: T.DD[:], [D], [], 5000)
    for k in range(16):
        b = blk(k)
        o, a = ("RT", k, 256, 16), (EB, 16 + 16 * b, 32 + 16 * b)
        if k % 2:
            act(o, a, F.Copy)
        else:
            cp(o, a)
        ops[-1]["wr"] = [("RT", 3000 + k, 3001 + k)]
    add("v", lambda e: e.transpose(T.XF[:, 0:256], T.RT[:, 0:256]), [("RT", 3000, 3016)], [("XF", 0, 256)], cost1(256, False))
    for b in range(8):
        add("v", (lambda b: lambda e: e.tensor_scalar(T.YI[:, b], T.XF[:, 32 * b:32 * b + 32], -1184.0, None, A.add))(b),
            [("XF", 32 * b, 32 * b + 32)], [("YI", 32 * b, 32 * b + 32)], cost1(32, False))
        add("s", (lambda b: lambda e: e.activation(T.YJ[:, b], T.XF[:, 32 * b:32 * b + 32], F.Identity, bias=-1184.0))(b),
            [("XF", 32 * b, 32 * b + 32)], [("YJ", 32 * b, 32 * b + 32), ("YJ", 1000 + 32 * b, 1032 + 32 * b)], 80 + CY * 64)
    for gi in range(8):
        o = gi ^ 1
        h = gi % 2
        dma("y", (lambda gi, o, h: lambda: T.YJ[16 * gi:16 * gi + 16, :, 16 * (1 - h):16 * (1 - h) + 16])(gi, o, h),
            (lambda gi, o, h: lambda: T.YI[16 * o:16 * o + 16, :, 16 * h:16 * h + 16])(gi, o, h),
            [("YI", 0, 256), ("YJ", 0, 256)], [("YJ", 2000 + gi, 2001 + gi)], 1900)
    dma("y", lambda: T.ye[:], lambda: T.YJ[:], [("YJ", 0, 256), ("YJ", 2000, 2008)], [], 2000)
    return ops


def depend(ops):
    hist = {}
    deps = []
    for i, op in enumerate(ops):
        need = set()
        for rw, regs in ((0, op["rd"]), (1, op["wr"])):
            for name, lo, hi in regs:
                bank = name in PSUM
                for j, jw, jlo, jhi in hist.get(name, ()):
                    if ((jw or rw) and jlo < hi and lo < jhi) or (bank and ops[j]["q"] != op["q"]):
                        need.add(j)
        for name, lo, hi in op["wr"]:
            if name not in PSUM:
                hist[name] = [x for x in hist.get(name, []) if not (lo <= x[2] and x[3] <= hi)]
        for rw, regs in ((0, op["rd"]), (1, op["wr"])):
            for name, lo, hi in regs:
                hist.setdefault(name, []).append((i, rw, lo, hi))
                if name in PSUM and len(hist[name]) > 160:
                    hist[name] = hist[name][-160:]
        need.discard(i)
        deps.append(sorted(need))
    return deps


def schedule(ops, deps):
    n = len(ops)
    succ = [[] for _ in range(n)]
    alld = []
    for i in range(n):
        d = list(deps[i])
        if ops[i]["after"] is not None:
            d.append(ops[i]["after"])
        alld.append(d)
        for j in d:
            succ[j].append(i)
    pri = [0.0] * n
    for i in range(n - 1, -1, -1):
        m = 0.0
        for j in succ[i]:
            m = max(m, pri[j] + WAKE)
        pri[i] = m + ops[i]["cost"] + ops[i]["lat"]
    pri = [pri[i] + BONUS.get(ops[i]["cls"], 0.0) for i in range(n)]
    left = [len(d) for d in alld]
    est = [0.0] * n
    free = {}
    ready = {}
    for i in range(n):
        if left[i] == 0:
            ready.setdefault(ops[i]["q"], []).append(i)
    order = []
    start = [0.0] * n
    while len(order) < n:
        best = None
        for q, lst in ready.items():
            if not lst:
                continue
            f = free.get(q, 0.0)
            t0 = max(f, min(est[i] for i in lst))
            c = max((i for i in lst if est[i] <= t0), key=lambda i: pri[i])
            if best is None or (t0, -pri[c]) < best[0]:
                best = ((t0, -pri[c]), q, c)
        (t0, _p), q, c = best
        ready[q].remove(c)
        start[c] = t0
        order.append(c)
        free[q] = t0 + ops[c]["cost"]
        for j in succ[c]:
            e = t0 + ops[c]["cost"] + (0.0 if ops[j]["after"] == c else ops[c]["lat"] + WAKE)
            est[j] = max(est[j], e)
            left[j] -= 1
            if left[j] == 0:
                ready.setdefault(ops[j]["q"], []).append(j)
    return order, start, max(start[i] + ops[i]["cost"] + ops[i]["lat"] for i in range(n))


def emit(g, T, ops, deps, order):
    eng = {"v": g.vector, "s": g.scalar, "t": g.tensor, "g": g, "y": g.sync}
    qsem = {"v": "qv", "s": "qs", "t": "qt", "g": "qg"}
    count = {}
    know = {q: {} for q in eng}
    waited = {}
    total = {}
    clock = [None] * len(ops)
    token = [None] * len(ops)
    for i in order:
        op = ops[i]
        q = op["q"]
        if op["kind"] == "arr":
            token[i] = (op["sem"], 16)
            clock[i] = {op["sem"]: 16}
            total[op["sem"]] = 16
            continue
        K = know[q]
        ds = sorted(deps[i], key=lambda j: -sum(clock[j].values()))
        for j in ds:
            s, v = token[j]
            if K.get(s, 0) >= v:
                continue
            eng[q].wait_ge(T.sem[s], v)
            waited[s] = max(waited.get(s, 0), v)
            for a, b in clock[j].items():
                if K.get(a, 0) < b:
                    K[a] = b
        ins = op["fn"](eng[q])
        if op["kind"] == "c":
            s = qsem[q]
            count[s] = count.get(s, 0) + 1
            ins.then_inc(T.sem[s], 1)
            token[i] = (s, count[s])
        else:
            if op["kind"] == "dma":
                ins.then_inc(T.sem[op["sem"]], 16)
            token[i] = (op["sem"], 16)
        total[token[i][0]] = token[i][1]
        c = dict(K)
        c[token[i][0]] = token[i][1]
        clock[i] = c
    for s, v in total.items():
        if waited.get(s, 0) < v:
            g.wait_ge(T.sem[s], v)


def rank_program(g, core, T, topo):
    if T.rank_of(core) is None:
        return
    ops = build(T, core, topo)
    deps = depend(ops)
    order, start, span = schedule(ops, deps)
    emit(g, T, ops, deps, order)
